import numpy as np, ml_dtypes
CORES = [169,41,209,81,249,121]
N = 6
DEAD = {"mate_links":[[15,0]],"switch_ports":[[5,0],[5,1]],"chips":[]}
def setup_inputs(rng):
    return {"x": rng.standard_normal((N, 128, 96), dtype=np.float32).astype(ml_dtypes.bfloat16)}
def reference(x):
    b = 96 // N
    blocks = x.reshape(N, 128, N, b)
    return {"y": np.ascontiguousarray(blocks.transpose(2, 1, 0, 3)).reshape(N, 128, 96)}

@@ -1,0 +1,125 @@
+from concourse.bass import DstId, RemoteDMATransfer
+
+N = 6
+B = 16
+
+SCRATCH = {
+    "out": ("dram", [N, 128, B], "bfloat16"),
+    "land": ("dram", [N, 128, B], "bfloat16"),
+}
+SEMAPHORES = ["l0", "l1", "l2", "a0", "a1", "a2", "a3", "a4", "a5", "sent", "st"]
+
+
+def _ways(cores):
+    chip = [c // 8 for c in cores]
+    hub = chip[1] ^ 1
+    far = (0, 4, 5)
+    to_hub = {0: (2, 2), 4: (6, 6), 5: (2, 3)}
+    from_hub = {0: (2, 2), 4: (6, 6), 5: (3, 2)}
+    to_even = {0: (3, 6), 4: (2, 3), 5: (3, 3), 1: (7, 7)}
+    to_odd = {0: 2, 4: 3, 5: 6}
+    ways = {}
+    for s in range(N):
+        for d in range(N):
+            if s == d:
+                continue
+            via = []
+            if chip[s] % 2 != chip[d] % 2:
+                if d == 1:
+                    via = [hub * 8 + 7]
+                elif chip[s] % 2:
+                    via = [chip[s] * 8 + to_even[s][d - 2]]
+                else:
+                    via = [chip[s] * 8 + to_odd[d]]
+            elif d == 1:
+                via = [chip[s] * 8 + to_hub[s][0], hub * 8 + to_hub[s][1]]
+            elif s == 1:
+                via = [chip[s] * 8 + from_hub[d][0], (chip[d] ^ 1) * 8 + from_hub[d][1]]
+            ways[(s, d)] = [cores[s]] + via + [cores[d]]
+    return ways
+
+
+def _masks(src, dsts):
+    off = [d // 8 != src // 8 for d in dsts]
+    p = 1
+    while p < len(dsts):
+        p *= 2
+    w = (8 if all(off) else 16) // p
+    assert sum(off) * w <= 8
+    return [(((1 << w) - 1) << (i * w), w) for i in range(len(dsts))]
+
+
+def _plan(cores):
+    ways = _ways(cores)
+    raw, slots = {}, {}
+    for (s, d), w in sorted(ways.items()):
+        at = d
+        for i in range(len(w) - 1):
+            last = i == len(w) - 2
+            if last:
+                nxt, sm = s, s
+            else:
+                nxt, sm = slots.get(w[i + 1], 0), 0
+                slots[w[i + 1]] = nxt + 1
+            cls = (3 - (len(w) - 1)) if i == 0 else 0
+            raw.setdefault(w[i], {}).setdefault(cls, []).append((at, w[i + 1], nxt, sm))
+            at = nxt
+    calls, due = {}, {}
+    for c, by in raw.items():
+        calls[c] = []
+        for cls in sorted(by):
+            items = sorted(by[cls], key=lambda it: it[1] // 8 == c // 8)
+            ms = _masks(c, [it[1] for it in items])
+            call = [it + m for it, m in zip(items, ms)]
+            calls[c].append(call)
+            for it in call:
+                dd = due.setdefault(it[1], {})
+                dd[it[3]] = dd.get(it[3], 0) + it[5]
+    return calls, due, {k: len(w) - 1 for k, w in ways.items()}
+
+
+def rank_program(g, core, T, topo):
+    calls, due, hops = _plan(list(T.cores))
+    if core not in calls:
+        return
+    sem = T.sem
+    rank = T.rank_of(core)
+    src = T.out if rank is not None else T.land
+    left = [0]
+
+    def fire(call):
+        trs = []
+        for (at, dst, slot, sm, mask, w) in call:
+            rid, pid = topo.addr(dst, core)
+            left[0] += w
+            if len(call) == 1:
+                g.remote_dma(out_ap=T.land[slot], in_ap=src[at], remote_sem=sem["a%d" % sm], local_sem=sem.sent,
+                             pid=pid, routing_id=rid, dma_engine_mask=mask)
+                return
+            trs.append(RemoteDMATransfer(dst_ids=[DstId(rid=rid, pnc=pid)], dma_engine_mask=mask,
+                                         remote_sem=sem["a%d" % sm], src=src[at], dst=T.land[slot]))
+        g.remote_dma_fused(trs, local_sem=sem.sent)
+
+    if rank is None:
+        g.wait_ge(sem.a0, due[core][0])
+        fire(calls[core][0])
+        g.wait_ge(sem.sent, left[0])
+        return
+
+    q = [g.sync, g.scalar]
+    n = 0
+    for k, call in enumerate(calls[core]):
+        for it in call:
+            d = it[0]
+            q[n % 2].dma_start(T.out[d], T.x[:, d * B:(d + 1) * B]).then_inc(sem["l%d" % k], 16)
+            n += 1
+    q[n % 2].dma_start(T.y[:, rank * B:(rank + 1) * B], T.x[:, rank * B:(rank + 1) * B]).then_inc(sem.st, 16)
+    for k, call in enumerate(calls[core]):
+        g.wait_ge(sem["l%d" % k], 16 * len(call))
+        fire(call)
+    order = sorted((s for s in range(N) if s != rank), key=lambda s: (hops[(s, rank)], s))
+    for k, s in enumerate(order):
+        q[k % 2].wait_ge(sem["a%d" % s], due[core][s])
+        q[k % 2].dma_start(T.y[:, s * B:(s + 1) * B], T.land[s]).then_inc(sem.st, 16)
+    g.wait_ge(sem.sent, left[0])
+    g.wait_ge(sem.st, 16 * N)

@@ -4,8 +4,10 @@ N = 6
 B = 16
 
 SCRATCH = {
-    "out": ("dram", [N, 128, B], "bfloat16"),
-    "land": ("dram", [N, 128, B], "bfloat16"),
+    "outS": ("dram", [N, 128, B], "bfloat16"),
+    "outP": ("dram", [N // 2, 128, 2 * B], "bfloat16"),
+    "landS": ("dram", [N, 128, B], "bfloat16"),
+    "landP": ("dram", [N, 128, 2 * B], "bfloat16"),
 }
 SEMAPHORES = ["l0", "l1", "l2", "a0", "a1", "a2", "a3", "a4", "a5", "sent", "st"]
 
@@ -13,9 +15,8 @@ SEMAPHORES = ["l0", "l1", "l2", "a0", "a1", "a2", "a3", "a4", "a5", "sent", "st"
 def _ways(cores):
     chip = [c // 8 for c in cores]
     hub = chip[1] ^ 1
-    far = (0, 4, 5)
     to_hub = {0: (2, 2), 4: (6, 6), 5: (2, 3)}
-    from_hub = {0: (2, 2), 4: (6, 6), 5: (3, 2)}
+    from_hub = {0: (2, 2), 4: (3, 2), 5: (3, 2)}
     to_even = {0: (3, 6), 4: (2, 3), 5: (3, 3), 1: (7, 7)}
     to_odd = {0: 2, 4: 3, 5: 6}
     ways = {}
@@ -39,6 +40,18 @@ def _ways(cores):
     return ways
 
 
+def _paired(s, d):
+    return s == 1 and d != 0
+
+
+def _turn(s, d):
+    if s == 1:
+        return {4: 0, 5: 0, 0: 1, 2: 2, 3: 2}[d]
+    if d == 1:
+        return 0
+    return 1 if (s in (2, 3)) != (d in (2, 3)) else 2
+
+
 def _masks(src, dsts):
     off = [d // 8 != src // 8 for d in dsts]
     p = 1
@@ -53,28 +66,32 @@ def _plan(cores):
     ways = _ways(cores)
     raw, slots = {}, {}
     for (s, d), w in sorted(ways.items()):
-        at = d
+        form = "P" if _paired(s, d) else "S"
+        first = d // 2 if form == "P" else d
+        frm, at = "out" + form, first
         for i in range(len(w) - 1):
-            last = i == len(w) - 2
-            if last:
+            to = "land" + form
+            if i == len(w) - 2:
                 nxt, sm = s, s
             else:
-                nxt, sm = slots.get(w[i + 1], 0), 0
-                slots[w[i + 1]] = nxt + 1
-            cls = (3 - (len(w) - 1)) if i == 0 else 0
-            raw.setdefault(w[i], {}).setdefault(cls, []).append((at, w[i + 1], nxt, sm))
-            at = nxt
+                mine = slots.setdefault(w[i + 1], {})
+                nxt, sm = mine.setdefault((s, form, first), len(mine)), 0
+            cls = _turn(s, d) if i == 0 else 0
+            lst = raw.setdefault(w[i], {}).setdefault(cls, [])
+            if (frm, at, w[i + 1], to, nxt, sm) not in lst:
+                lst.append((frm, at, w[i + 1], to, nxt, sm))
+            frm, at = to, nxt
     calls, due = {}, {}
     for c, by in raw.items():
         calls[c] = []
         for cls in sorted(by):
-            items = sorted(by[cls], key=lambda it: it[1] // 8 == c // 8)
-            ms = _masks(c, [it[1] for it in items])
+            items = sorted(by[cls], key=lambda it: it[2] // 8 == c // 8)
+            ms = _masks(c, [it[2] for it in items])
             call = [it + m for it, m in zip(items, ms)]
             calls[c].append(call)
             for it in call:
-                dd = due.setdefault(it[1], {})
-                dd[it[3]] = dd.get(it[3], 0) + it[5]
+                dd = due.setdefault(it[2], {})
+                dd[it[5]] = dd.get(it[5], 0) + it[7]
     return calls, due, {k: len(w) - 1 for k, w in ways.items()}
 
 
@@ -84,20 +101,19 @@ def rank_program(g, core, T, topo):
         return
     sem = T.sem
     rank = T.rank_of(core)
-    src = T.out if rank is not None else T.land
     left = [0]
 
     def fire(call):
         trs = []
-        for (at, dst, slot, sm, mask, w) in call:
+        for (frm, at, dst, to, slot, sm, mask, w) in call:
             rid, pid = topo.addr(dst, core)
             left[0] += w
             if len(call) == 1:
-                g.remote_dma(out_ap=T.land[slot], in_ap=src[at], remote_sem=sem["a%d" % sm], local_sem=sem.sent,
+                g.remote_dma(out_ap=T[to][slot], in_ap=T[frm][at], remote_sem=sem["a%d" % sm], local_sem=sem.sent,
                              pid=pid, routing_id=rid, dma_engine_mask=mask)
                 return
             trs.append(RemoteDMATransfer(dst_ids=[DstId(rid=rid, pnc=pid)], dma_engine_mask=mask,
-                                         remote_sem=sem["a%d" % sm], src=src[at], dst=T.land[slot]))
+                                         remote_sem=sem["a%d" % sm], src=T[frm][at], dst=T[to][slot]))
         g.remote_dma_fused(trs, local_sem=sem.sent)
 
     if rank is None:
@@ -108,18 +124,22 @@ def rank_program(g, core, T, topo):
 
     q = [g.sync, g.scalar]
     n = 0
-    for k, call in enumerate(calls[core]):
-        for it in call:
-            d = it[0]
-            q[n % 2].dma_start(T.out[d], T.x[:, d * B:(d + 1) * B]).then_inc(sem["l%d" % k], 16)
+    loads = [sorted(set((it[0], it[1]) for it in call)) for call in calls[core]]
+    for k, srcs in enumerate(loads):
+        for buf, at in srcs:
+            wd = 2 * B if buf == "outP" else B
+            q[n % 2].dma_start(T[buf][at], T.x[:, at * wd:(at + 1) * wd]).then_inc(sem["l%d" % k], 16)
             n += 1
     q[n % 2].dma_start(T.y[:, rank * B:(rank + 1) * B], T.x[:, rank * B:(rank + 1) * B]).then_inc(sem.st, 16)
     for k, call in enumerate(calls[core]):
-        g.wait_ge(sem["l%d" % k], 16 * len(call))
+        g.wait_ge(sem["l%d" % k], 16 * len(loads[k]))
         fire(call)
+
     order = sorted((s for s in range(N) if s != rank), key=lambda s: (hops[(s, rank)], s))
+    h = rank % 2
     for k, s in enumerate(order):
         q[k % 2].wait_ge(sem["a%d" % s], due[core][s])
-        q[k % 2].dma_start(T.y[:, s * B:(s + 1) * B], T.land[s]).then_inc(sem.st, 16)
+        got = T.landP[s, :, h * B:(h + 1) * B] if _paired(s, rank) else T.landS[s]
+        q[k % 2].dma_start(T.y[:, s * B:(s + 1) * B], got).then_inc(sem.st, 16)
     g.wait_ge(sem.sent, left[0])
     g.wait_ge(sem.st, 16 * N)

from concourse.bass import DstId, RemoteDMATransfer

N = 6
B = 16

SCRATCH = {
    "outS": ("dram", [N, 128, B], "bfloat16"),
    "outP": ("dram", [N // 2, 128, 2 * B], "bfloat16"),
    "landS": ("dram", [N, 128, B], "bfloat16"),
    "landP": ("dram", [N, 128, 2 * B], "bfloat16"),
}
SEMAPHORES = ["l0", "l1", "l2", "a0", "a1", "a2", "a3", "a4", "a5", "sent", "st"]


def _ways(cores):
    chip = [c // 8 for c in cores]
    hub = chip[1] ^ 1
    to_hub = {0: (2, 2), 4: (6, 6), 5: (2, 3)}
    from_hub = {0: (2, 2), 4: (3, 2), 5: (3, 2)}
    to_even = {0: (3, 6), 4: (2, 3), 5: (3, 3), 1: (7, 7)}
    to_odd = {0: 2, 4: 3, 5: 6}
    ways = {}
    for s in range(N):
        for d in range(N):
            if s == d:
                continue
            via = []
            if chip[s] % 2 != chip[d] % 2:
                if d == 1:
                    via = [hub * 8 + 7]
                elif chip[s] % 2:
                    via = [chip[s] * 8 + to_even[s][d - 2]]
                else:
                    via = [chip[s] * 8 + to_odd[d]]
            elif d == 1:
                via = [chip[s] * 8 + to_hub[s][0], hub * 8 + to_hub[s][1]]
            elif s == 1:
                via = [chip[s] * 8 + from_hub[d][0], (chip[d] ^ 1) * 8 + from_hub[d][1]]
            ways[(s, d)] = [cores[s]] + via + [cores[d]]
    return ways


def _paired(s, d):
    return s == 1 and d != 0


def _turn(s, d):
    if s == 1:
        return {4: 0, 5: 0, 0: 1, 2: 2, 3: 2}[d]
    if d == 1:
        return 0
    return 1 if (s in (2, 3)) != (d in (2, 3)) else 2


def _masks(src, dsts):
    off = [d // 8 != src // 8 for d in dsts]
    p = 1
    while p < len(dsts):
        p *= 2
    w = (8 if all(off) else 16) // p
    assert sum(off) * w <= 8
    return [(((1 << w) - 1) << (i * w), w) for i in range(len(dsts))]


def _plan(cores):
    ways = _ways(cores)
    raw, slots = {}, {}
    for (s, d), w in sorted(ways.items()):
        form = "P" if _paired(s, d) else "S"
        first = d // 2 if form == "P" else d
        frm, at = "out" + form, first
        for i in range(len(w) - 1):
            to = "land" + form
            if i == len(w) - 2:
                nxt, sm = s, s
            else:
                mine = slots.setdefault(w[i + 1], {})
                nxt, sm = mine.setdefault((s, form, first), len(mine)), 0
            cls = _turn(s, d) if i == 0 else 0
            lst = raw.setdefault(w[i], {}).setdefault(cls, [])
            if (frm, at, w[i + 1], to, nxt, sm) not in lst:
                lst.append((frm, at, w[i + 1], to, nxt, sm))
            frm, at = to, nxt
    calls, due = {}, {}
    for c, by in raw.items():
        calls[c] = []
        for cls in sorted(by):
            items = sorted(by[cls], key=lambda it: it[2] // 8 == c // 8)
            ms = _masks(c, [it[2] for it in items])
            call = [it + m for it, m in zip(items, ms)]
            calls[c].append(call)
            for it in call:
                dd = due.setdefault(it[2], {})
                dd[it[5]] = dd.get(it[5], 0) + it[7]
    return calls, due, {k: len(w) - 1 for k, w in ways.items()}


def rank_program(g, core, T, topo):
    calls, due, hops = _plan(list(T.cores))
    if core not in calls:
        return
    sem = T.sem
    rank = T.rank_of(core)
    left = [0]

    def fire(call):
        trs = []
        for (frm, at, dst, to, slot, sm, mask, w) in call:
            rid, pid = topo.addr(dst, core)
            left[0] += w
            if len(call) == 1:
                g.remote_dma(out_ap=T[to][slot], in_ap=T[frm][at], remote_sem=sem["a%d" % sm], local_sem=sem.sent,
                             pid=pid, routing_id=rid, dma_engine_mask=mask)
                return
            trs.append(RemoteDMATransfer(dst_ids=[DstId(rid=rid, pnc=pid)], dma_engine_mask=mask,
                                         remote_sem=sem["a%d" % sm], src=T[frm][at], dst=T[to][slot]))
        g.remote_dma_fused(trs, local_sem=sem.sent)

    if rank is None:
        g.wait_ge(sem.a0, due[core][0])
        fire(calls[core][0])
        g.wait_ge(sem.sent, left[0])
        return

    q = [g.sync, g.scalar]
    n = 0
    loads = [sorted(set((it[0], it[1]) for it in call)) for call in calls[core]]
    for k, srcs in enumerate(loads):
        for buf, at in srcs:
            wd = 2 * B if buf == "outP" else B
            q[n % 2].dma_start(T[buf][at], T.x[:, at * wd:(at + 1) * wd]).then_inc(sem["l%d" % k], 16)
            n += 1
    q[n % 2].dma_start(T.y[:, rank * B:(rank + 1) * B], T.x[:, rank * B:(rank + 1) * B]).then_inc(sem.st, 16)
    for k, call in enumerate(calls[core]):
        g.wait_ge(sem["l%d" % k], 16 * len(loads[k]))
        fire(call)

    order = sorted((s for s in range(N) if s != rank), key=lambda s: (hops[(s, rank)], s))
    h = rank % 2
    for k, s in enumerate(order):
        q[k % 2].wait_ge(sem["a%d" % s], due[core][s])
        got = T.landP[s, :, h * B:(h + 1) * B] if _paired(s, rank) else T.landS[s]
        q[k % 2].dma_start(T.y[:, s * B:(s + 1) * B], got).then_inc(sem.st, 16)
    g.wait_ge(sem.sent, left[0])
    g.wait_ge(sem.st, 16 * N)
